import numpy as np
import ml_dtypes


def mxq(x, axis, fmt="e4m3"):
    dtype, down = {"e4m3": (ml_dtypes.float8_e4m3fn, 7), "e5m2": (ml_dtypes.float8_e5m2, 14)}[fmt]
    v = np.moveaxis(np.asarray(x, np.float32).astype(ml_dtypes.bfloat16).astype(np.float64), axis, -1)
    blocks = v.reshape(v.shape[:-1] + (-1, 32))
    amax = np.abs(blocks).max(-1, keepdims=True)
    byte = np.maximum(np.where(amax > 0, np.frexp(amax)[1] - 1 + 127, 0) - down, 1)
    scale = np.exp2(byte - 127.0)
    codes = (blocks / scale).astype(np.float32).astype(dtype).astype(np.float64)
    return np.moveaxis((codes * scale).reshape(v.shape), -1, axis)


WIDE = False


def mx_kscale(k):
    if not WIDE:
        return np.ones(k)
    levels = np.array([10, -10, 5, -5, 0])
    if k % 512:
        return np.exp2(np.random.permutation(np.resize(levels, k // 32))).repeat(32)
    a = np.empty((k // 512, 16))
    for p in range(k // 512):
        a[p, :8] = np.random.permutation(np.resize(levels, 8))
        for g in range(8):
            far = levels[np.abs(levels - a[p, g]) >= 10]
            a[p, g + 8] = far[np.random.randint(len(far))]
    return np.exp2(a.ravel()).repeat(32)


def f64(x):
    return np.asarray(x).astype(np.float64)


def striped(idx):
    return np.tile(np.asarray(idx).reshape(-1, 16).T, (8, 1)).astype(np.uint16)


def unstriped(offs):
    return offs[:16].T.reshape(-1).astype(np.int64)


E2M1 = np.array([0.0, 0.5, 1.0, 1.5, 2.0, 3.0, 4.0, 6.0, -0.0, -0.5, -1.0, -1.5, -2.0, -3.0, -4.0, -6.0])


def pack_weight(w, fmt):
    k, n = w.shape
    w = f64(np.asarray(w, np.float32).astype(ml_dtypes.bfloat16)).reshape(k // 32, 32, n)
    amax = np.abs(w).max(1)
    if fmt == "e4m3":
        byte = np.frexp(amax)[1] - 1 + 127 - 7
    else:
        mant, ex = np.frexp(amax / 6.0)
        byte = np.where(mant > 0.5, ex, ex - 1) + 127
    byte = np.clip(np.where(amax > 0, byte, 1), 1, 254)
    scaled = (w * np.exp2(127.0 - byte)[:, None, :]).reshape(k, n).astype(np.float32)
    by_word = np.ascontiguousarray(scaled.reshape(k // 512, 128, 4, n).transpose(0, 1, 3, 2))
    if fmt == "e4m3":
        words = by_word.astype(ml_dtypes.float8_e4m3fn).view(np.uint8)
    else:
        c = by_word.astype(ml_dtypes.float4_e2m1fn).view(np.uint8) & 0xF
        words = (c[..., 0::2] | (c[..., 1::2] << 4)).reshape(k // 512, 128, 2 * n)
    return np.ascontiguousarray(words), np.ascontiguousarray(byte.astype(np.uint8).reshape(k // 512, 16, n))


def unpack_weight(words, scales, fmt):
    g, _, n = scales.shape
    words = np.ascontiguousarray(words).reshape(g, 128, n, -1)
    if fmt == "e4m3":
        vals = words.view(ml_dtypes.float8_e4m3fn).astype(np.float64)
    else:
        nib = np.empty((g, 128, n, 4), np.uint8)
        nib[..., 0::2] = words & 0xF
        nib[..., 1::2] = words >> 4
        vals = E2M1[nib]
    vals = vals * np.repeat(np.exp2(scales.astype(np.float64) - 127.0), 8, axis=1)[..., None]
    return vals.transpose(0, 1, 3, 2).reshape(g * 512, n)


D, T, I, Q, E = 512, 2048, 512, 128, 512


def setup_inputs():
    n = np.random.standard_normal
    idx = np.random.permutation(T)[:I]
    fd = mx_kscale(D)
    fi = mx_kscale(I)
    ti = np.ones(T)
    ti[idx] = fi
    keysp = pack_weight(n((D, T)) / fd[:, None], "e4m3")
    return {
        "query": (n((D, Q)) * 1.0 / np.sqrt(D) * fd[:, None]).astype(np.float32),
        "keys_words": keysp[0],
        "keys_scales": keysp[1],
        "cap": (np.random.uniform(0.002, 0.004, (Q, 1))).astype(np.float32),
        "stand": (1.0 * n((1, E))).astype(np.float32),
        "size": (np.random.uniform(0.5, 2.0, (1, I)) * fi).astype(np.float32),
        "vals": (n((E, T)) / ti).astype(np.float32),
        "offs": striped(idx),
    }


def reference(query, keys_words, keys_scales, cap, stand, size, vals, offs):
    idx = unstriped(offs)
    keysu = unpack_weight(keys_words, keys_scales, "e4m3")
    queryq = mxq(f64(query), 0, "e4m3")
    keysidxg = keysu[:, idx]
    a = queryq.T @ keysidxg
    p = np.exp(a - np.max(a, axis=1, keepdims=True))
    c1 = np.minimum(p / np.sum(p, axis=1, keepdims=True), f64(cap))
    left = np.sum(c1, axis=1, keepdims=True) * (-1.0) + 1.0
    w = c1 * f64(size)
    wt = w.T
    vt = f64(vals)[:, idx].T
    wtq = mxq(wt, 0, "e4m3")
    vtq = mxq(vt, 0, "e4m3")
    o = wtq.T @ vtq
    y = o + f64(stand) * left
    return y

@@ -1,0 +1,175 @@
+from contextlib import ExitStack
+
+import concourse.mybir as mybir
+from concourse.masks import make_identity
+
+D, T, I, Q, E = 512, 2048, 512, 128, 512
+FLOPS = 2 * Q * I * D + 2 * Q * E * I
+
+F32 = mybir.dt.float32
+BF16 = mybir.dt.bfloat16
+I32 = mybir.dt.int32
+U32 = mybir.dt.uint32
+U16 = mybir.dt.uint16
+U8 = mybir.dt.uint8
+FP8X4 = mybir.dt.float8_e4m3fn_x4
+ALU = mybir.AluOpType
+ACT = mybir.ActivationFunctionType
+AX = mybir.AxisListType
+
+P = 128
+PACK = 4
+BLOCKS = E // P
+
+
+def tile_attend_cappedweights_kernel(tc, query, keys_words, keys_scales, cap, stand, size, vals, offs, out):
+    nc = tc.nc
+    with ExitStack() as ctx:
+        keep = ctx.enter_context(tc.tile_pool(name="keep", bufs=1))
+        psum = ctx.enter_context(tc.psum_pool(name="psum", bufs=1))
+
+        offsets = keep.tile([P, I // 16], U16, name="offsets")
+        nc.sync.dma_start(offsets[:], offs)
+
+        key_scale_pool = keep.tile([P, T], U8, name="key_scale_pool", align_bytes=64)
+        for quad in range(4):
+            rows = keys_scales[0:1, 4 * quad : 4 * quad + 4, :].bitcast(I32)
+            nc.sync.dma_start(
+                key_scale_pool[32 * quad : 32 * quad + 32, :].bitcast(I32),
+                rows.to_broadcast([8, 4, T // 4]),
+            )
+
+        query_raw = keep.tile([P, PACK, Q], F32, name="query_raw")
+        nc.sync.dma_start(query_raw[:], query.rearrange("(p j) q -> p j q", j=PACK))
+        key_word_pool = keep.tile([P, T], I32, name="key_word_pool", align_bytes=64)
+        nc.sync.dma_start(key_word_pool[:], keys_words[0].rearrange("p n t -> p (n t)").bitcast(I32))
+
+        val_pool = []
+
+        def load_vals(b):
+            pool_b = keep.tile([P, T], F32, name="val_pool%d" % b, tag="val_pool%d" % b, align_bytes=64)
+            nc.sync.dma_start(pool_b[:], vals[b * P : (b + 1) * P, :])
+            val_pool.append(pool_b)
+
+        load_vals(0)
+        cap_col = keep.tile([P, 1], F32, name="cap_col")
+        nc.sync.dma_start(cap_col[:], cap)
+        size4 = keep.tile([P, PACK], F32, name="size4")
+        nc.sync.dma_start(size4[:], size.rearrange("o (p t) -> (o p) t", t=PACK))
+        stand4 = keep.tile([P, PACK], F32, name="stand4")
+        nc.sync.dma_start(stand4[:], stand.rearrange("o (p t) -> (o p) t", t=PACK))
+        for b in range(1, BLOCKS):
+            load_vals(b)
+
+        ident = keep.tile([P, P], F32, name="ident")
+        make_identity(nc, ident[:])
+
+        key_scales = keep.tile([P, I], U8, name="key_scales", align_bytes=64)
+        nc.vector.tensor_copy(key_scales[:], key_scale_pool[:].indirect(offsets[:]))
+
+        query_bf = keep.tile([P, Q, PACK], BF16, name="query_bf", align_bytes=64)
+        nc.scalar.copy(query_bf[:], query_raw[:].rearrange("p j q -> p q j"))
+        query_words = keep.tile([P, Q], U32, name="query_words", align_bytes=64)
+        query_scales = keep.tile([P, Q], U8, name="query_scales", align_bytes=64)
+        nc.vector.quantize_mx(query_words[:].bitcast(FP8X4), query_scales[:], query_bf[:].rearrange("p q j -> p (q j)"))
+
+        key_words = keep.tile([P, I], U32, name="key_words", align_bytes=64)
+        nc.vector.tensor_copy(key_words[:], key_word_pool[:].bitcast(U32).indirect(offsets[:]))
+
+        scores = psum.tile([P, I], F32, name="scores")
+        nc.tensor.matmul_mx(
+            scores[:], lhsT=query_words[:].bitcast(FP8X4), lhsT_scale=query_scales[:],
+            rhs=key_words[:].bitcast(FP8X4), rhs_scale=key_scales[:], start=True, stop=True,
+        )
+
+        stand_ps = psum.tile([P, PACK, P], F32, name="stand_ps")
+        for j in range(PACK):
+            nc.tensor.transpose(stand_ps[:, j, :], stand4[:, j : j + 1].to_broadcast([P, P]), ident[:])
+        stand_rows = keep.tile([P, P, PACK], F32, name="stand_rows")
+        nc.scalar.copy(stand_rows[:], stand_ps[:].rearrange("q j n -> q n j"))
+
+        neg_max = keep.tile([P, 1], F32, name="neg_max")
+        nc.vector.tensor_reduce(neg_max[:], scores[:], AX.X, ALU.max, negate=True)
+        probs = keep.tile([P, PACK, P], F32, name="probs")
+        row_sum = keep.tile([P, 1], F32, name="row_sum")
+        nc.scalar.activation(
+            probs[:], scores[:].rearrange("q (s t) -> q t s", t=PACK), ACT.Exp, bias=neg_max[:], scale=1.0, accum_out=row_sum[:]
+        )
+
+        val_words = []
+        val_scales = []
+
+        def gather_vals(b):
+            picked = keep.tile([P, I], BF16, name="picked%d" % b, align_bytes=64)
+            nc.vector.tensor_copy(picked[:], val_pool[b][:].indirect(offsets[:]))
+            pairs = picked[:].bitcast(F32)
+            turned = psum.tile([P, 2, P], F32, name="turned", tag="turned", bufs=2)
+            for u in range(2):
+                nc.tensor.transpose(turned[:, u, :], pairs[:, u : I // 2 : 2], ident[:])
+            grouped = keep.tile([P, P * PACK], BF16, name="grouped%d" % b, tag="grouped%d" % b, align_bytes=64)
+            nc.scalar.copy(
+                grouped[:].bitcast(F32).rearrange("p (e u) -> p e u", u=2), turned[:].rearrange("p u e -> p e u")
+            )
+            return grouped
+
+        def quantize_vals(b, grouped):
+            tag = "val_pool%d" % (b + 1) if 0 < b < BLOCKS - 1 else "val_words%d" % b
+            words = keep.tile([P, P], U32, name="val_words%d" % b, tag=tag, align_bytes=64)
+            scales = keep.tile([P, P], U8, name="val_scales%d" % b, align_bytes=64)
+            nc.vector.quantize_mx(words[:].bitcast(FP8X4), scales[:], grouped[:])
+            val_words.append(words)
+            val_scales.append(scales)
+
+        grouped0 = gather_vals(0)
+
+        inv_sum = keep.tile([P, 1], F32, name="inv_sum", tag="val_pool0", align_bytes=64)
+        nc.vector.reciprocal(inv_sum[:], row_sum[:])
+        capped = keep.tile([P, PACK, P], F32, name="capped")
+        nc.vector.tensor_scalar(capped[:], probs[:], inv_sum[:], cap_col[:], ALU.mult, ALU.min)
+        capped_t = psum.tile([P, PACK, P], F32, name="capped_t")
+        for t in range(PACK):
+            nc.tensor.transpose(capped_t[:, t, :], capped[:, t, :], ident[:])
+
+        quantize_vals(0, grouped0)
+        grouped1 = gather_vals(1)
+
+        weights_bf = keep.tile([P, Q, PACK], BF16, name="weights_bf", tag="val_pool1", align_bytes=64)
+        nc.vector.tensor_tensor(
+            weights_bf[:], capped_t[:].rearrange("p t q -> p q t"),
+            size4[:].unsqueeze(1).to_broadcast([P, Q, PACK]), ALU.mult,
+        )
+
+        neg_capped = keep.tile([P, PACK, P], F32, name="neg_capped")
+        neg_kept = keep.tile([P, 1], F32, name="neg_kept")
+        nc.scalar.activation(neg_capped[:], capped[:], ACT.Copy, scale=-1.0, accum_out=neg_kept[:])
+
+        weight_words = keep.tile([P, Q], U32, name="weight_words", align_bytes=64)
+        weight_scales = keep.tile([P, Q], U8, name="weight_scales", align_bytes=64)
+        nc.vector.quantize_mx(weight_words[:].bitcast(FP8X4), weight_scales[:], weights_bf[:].rearrange("p q t -> p (q t)"))
+        left = keep.tile([P, 1], F32, name="left")
+        nc.vector.tensor_scalar(left[:], neg_kept[:], 1.0, None, ALU.add)
+
+        stand_flat = stand_rows[:].rearrange("q n j -> q (n j)")
+
+        def finish(b):
+            acc = psum.tile([P, P], F32, name="acc", tag="acc", bufs=3)
+            nc.tensor.matmul_mx(
+                acc[:], lhsT=weight_words[:].bitcast(FP8X4), lhsT_scale=weight_scales[:],
+                rhs=val_words[b][:].bitcast(FP8X4), rhs_scale=val_scales[b][:], start=True, stop=True,
+            )
+            tag = "grouped%d" % (b + 1) if b + 2 < BLOCKS else "result%d" % b
+            result = keep.tile([P, P], F32, name="result%d" % b, tag=tag, align_bytes=64)
+            nc.vector.scalar_tensor_tensor(
+                result[:], stand_flat[:, b * P : (b + 1) * P], left[:], acc[:], ALU.mult, ALU.add
+            )
+            nc.sync.dma_start(out[:, b * P : (b + 1) * P], result[:])
+
+        grouped2 = gather_vals(2)
+        quantize_vals(1, grouped1)
+        finish(0)
+        grouped3 = gather_vals(3)
+        quantize_vals(2, grouped2)
+        finish(1)
+        finish(2)
+        quantize_vals(3, grouped3)
+        finish(3)

@@ -31,18 +31,19 @@ def tile_attend_cappedweights_kernel(tc, query, keys_words, keys_scales, cap, st
         offsets = keep.tile([P, I // 16], U16, name="offsets")
         nc.sync.dma_start(offsets[:], offs)
 
+        key_word_pool = keep.tile([P, T], I32, name="key_word_pool", align_bytes=64)
+        nc.sync.dma_start(key_word_pool[:], keys_words[0].rearrange("p n t -> p (n t)").bitcast(I32))
+
         key_scale_pool = keep.tile([P, T], U8, name="key_scale_pool", align_bytes=64)
-        for quad in range(4):
-            rows = keys_scales[0:1, 4 * quad : 4 * quad + 4, :].bitcast(I32)
+        nc.vector.memset(key_scale_pool[:].bitcast(I32), 0)
+        scale_rows = keys_scales[0].bitcast(I32)
+        for quad in (0, 2, 1, 3):
             nc.sync.dma_start(
-                key_scale_pool[32 * quad : 32 * quad + 32, :].bitcast(I32),
-                rows.to_broadcast([8, 4, T // 4]),
+                key_scale_pool[32 * quad : 32 * quad + 4, :].bitcast(I32), scale_rows[4 * quad : 4 * quad + 4, :]
             )
 
         query_raw = keep.tile([P, PACK, Q], F32, name="query_raw")
         nc.sync.dma_start(query_raw[:], query.rearrange("(p j) q -> p j q", j=PACK))
-        key_word_pool = keep.tile([P, T], I32, name="key_word_pool", align_bytes=64)
-        nc.sync.dma_start(key_word_pool[:], keys_words[0].rearrange("p n t -> p (n t)").bitcast(I32))
 
         val_pool = []
 
@@ -52,29 +53,27 @@ def tile_attend_cappedweights_kernel(tc, query, keys_words, keys_scales, cap, st
             val_pool.append(pool_b)
 
         load_vals(0)
-        cap_col = keep.tile([P, 1], F32, name="cap_col")
-        nc.sync.dma_start(cap_col[:], cap)
-        size4 = keep.tile([P, PACK], F32, name="size4")
-        nc.sync.dma_start(size4[:], size.rearrange("o (p t) -> (o p) t", t=PACK))
-        stand4 = keep.tile([P, PACK], F32, name="stand4")
-        nc.sync.dma_start(stand4[:], stand.rearrange("o (p t) -> (o p) t", t=PACK))
+        rows = keep.tile([P, P], F32, name="rows")
+        nc.gpsimd.memset(rows[:], 0.0)
+        nc.sync.dma_start(rows[8:9, :], cap.rearrange("q o -> o q"))
+        nc.sync.dma_start(rows[0:4, :], size.rearrange("o (a n) -> (o a) n", a=4))
+        nc.sync.dma_start(rows[4:8, :], stand.rearrange("o (a n) -> (o a) n", a=4))
         for b in range(1, BLOCKS):
             load_vals(b)
 
         ident = keep.tile([P, P], F32, name="ident")
         make_identity(nc, ident[:])
 
-        key_scales = keep.tile([P, I], U8, name="key_scales", align_bytes=64)
+        key_words = keep.tile([P, I], U32, name="key_words", align_bytes=64)
+        nc.vector.tensor_copy(key_words[:], key_word_pool[:].bitcast(U32).indirect(offsets[:]))
+        key_scales = keep.tile([P, I], U8, name="key_scales", tag="key_scales", align_bytes=64)
         nc.vector.tensor_copy(key_scales[:], key_scale_pool[:].indirect(offsets[:]))
 
         query_bf = keep.tile([P, Q, PACK], BF16, name="query_bf", align_bytes=64)
         nc.scalar.copy(query_bf[:], query_raw[:].rearrange("p j q -> p q j"))
-        query_words = keep.tile([P, Q], U32, name="query_words", align_bytes=64)
+        query_words = keep.tile([P, Q], U32, name="query_words", tag="query_words", align_bytes=64)
         query_scales = keep.tile([P, Q], U8, name="query_scales", align_bytes=64)
         nc.vector.quantize_mx(query_words[:].bitcast(FP8X4), query_scales[:], query_bf[:].rearrange("p q j -> p (q j)"))
-
-        key_words = keep.tile([P, I], U32, name="key_words", align_bytes=64)
-        nc.vector.tensor_copy(key_words[:], key_word_pool[:].bitcast(U32).indirect(offsets[:]))
 
         scores = psum.tile([P, I], F32, name="scores")
         nc.tensor.matmul_mx(
@@ -82,94 +81,91 @@ def tile_attend_cappedweights_kernel(tc, query, keys_words, keys_scales, cap, st
             rhs=key_words[:].bitcast(FP8X4), rhs_scale=key_scales[:], start=True, stop=True,
         )
 
-        stand_ps = psum.tile([P, PACK, P], F32, name="stand_ps")
-        for j in range(PACK):
-            nc.tensor.transpose(stand_ps[:, j, :], stand4[:, j : j + 1].to_broadcast([P, P]), ident[:])
-        stand_rows = keep.tile([P, P, PACK], F32, name="stand_rows")
-        nc.scalar.copy(stand_rows[:], stand_ps[:].rearrange("q j n -> q n j"))
-
         neg_max = keep.tile([P, 1], F32, name="neg_max")
         nc.vector.tensor_reduce(neg_max[:], scores[:], AX.X, ALU.max, negate=True)
-        probs = keep.tile([P, PACK, P], F32, name="probs")
-        row_sum = keep.tile([P, 1], F32, name="row_sum")
-        nc.scalar.activation(
-            probs[:], scores[:].rearrange("q (s t) -> q t s", t=PACK), ACT.Exp, bias=neg_max[:], scale=1.0, accum_out=row_sum[:]
-        )
+        probs = keep.tile([P, I], F32, name="probs")
+        row_sum = keep.tile([P, 1], F32, name="row_sum", tag="row_sum", align_bytes=64)
+        nc.scalar.activation(probs[:], scores[:], ACT.Exp, bias=neg_max[:], scale=1.0, accum_out=row_sum[:])
 
-        val_words = []
-        val_scales = []
+        rows_t = psum.tile([P, P], F32, name="rows_t", tag="bank0")
+        nc.tensor.transpose(rows_t[:], rows[:], ident[:])
+        cols = keep.tile([P, 16], F32, name="cols")
+        nc.scalar.copy(cols[:], rows_t[:, 0:16])
+        neg_cap = keep.tile([P, 1], F32, name="neg_cap")
+        nc.scalar.activation(neg_cap[:], rows_t[:, 8:9], ACT.Copy, scale=-1.0)
+        size_ps = psum.tile([P, I], F32, name="size_ps")
+        for a in range(4):
+            nc.tensor.transpose(size_ps[:, a * P : (a + 1) * P], cols[:, a : a + 1].to_broadcast([P, P]), ident[:])
 
-        def gather_vals(b):
-            picked = keep.tile([P, I], BF16, name="picked%d" % b, align_bytes=64)
-            nc.vector.tensor_copy(picked[:], val_pool[b][:].indirect(offsets[:]))
-            pairs = picked[:].bitcast(F32)
-            turned = psum.tile([P, 2, P], F32, name="turned", tag="turned", bufs=2)
+        def turn(flat, bank, grouped):
+            pairs = flat[:].bitcast(F32)
+            turned = psum.tile([P, 2, P], F32, name="turned", tag=bank)
             for u in range(2):
                 nc.tensor.transpose(turned[:, u, :], pairs[:, u : I // 2 : 2], ident[:])
-            grouped = keep.tile([P, P * PACK], BF16, name="grouped%d" % b, tag="grouped%d" % b, align_bytes=64)
             nc.scalar.copy(
-                grouped[:].bitcast(F32).rearrange("p (e u) -> p e u", u=2), turned[:].rearrange("p u e -> p e u")
+                grouped.bitcast(F32).rearrange("p (e u) -> p e u", u=2), turned[:].rearrange("p u e -> p e u")
             )
-            return grouped
 
-        def quantize_vals(b, grouped):
-            tag = "val_pool%d" % (b + 1) if 0 < b < BLOCKS - 1 else "val_words%d" % b
-            words = keep.tile([P, P], U32, name="val_words%d" % b, tag=tag, align_bytes=64)
-            scales = keep.tile([P, P], U8, name="val_scales%d" % b, align_bytes=64)
-            nc.vector.quantize_mx(words[:].bitcast(FP8X4), scales[:], grouped[:])
-            val_words.append(words)
-            val_scales.append(scales)
+        def gather_vals(b, tag):
+            picked = keep.tile([P, I], BF16, name="picked%d" % b, tag=tag, align_bytes=64)
+            nc.vector.tensor_copy(picked[:], val_pool[b][:].indirect(offsets[:]))
+            return picked
 
-        grouped0 = gather_vals(0)
+        def quantize(name, grouped, words):
+            scales = keep.tile(list(words.shape), U8, name=name + "_scales", align_bytes=64)
+            nc.vector.quantize_mx(words.bitcast(FP8X4), scales[:], grouped)
+            return words, scales
 
-        inv_sum = keep.tile([P, 1], F32, name="inv_sum", tag="val_pool0", align_bytes=64)
+        grouped01 = keep.tile([P, 2 * I], BF16, name="grouped01", align_bytes=64)
+        turn(gather_vals(0, "query_words"), "bank0", grouped01[:, 0:I])
+        turn(gather_vals(1, "key_scales"), "bank1", grouped01[:, I : 2 * I])
+
+        inv_sum = keep.tile([P, 1], F32, name="inv_sum", tag="val_pool1", align_bytes=64)
         nc.vector.reciprocal(inv_sum[:], row_sum[:])
-        capped = keep.tile([P, PACK, P], F32, name="capped")
-        nc.vector.tensor_scalar(capped[:], probs[:], inv_sum[:], cap_col[:], ALU.mult, ALU.min)
-        capped_t = psum.tile([P, PACK, P], F32, name="capped_t")
-        for t in range(PACK):
-            nc.tensor.transpose(capped_t[:, t, :], capped[:, t, :], ident[:])
-
-        quantize_vals(0, grouped0)
-        grouped1 = gather_vals(1)
-
-        weights_bf = keep.tile([P, Q, PACK], BF16, name="weights_bf", tag="val_pool1", align_bytes=64)
-        nc.vector.tensor_tensor(
-            weights_bf[:], capped_t[:].rearrange("p t q -> p q t"),
-            size4[:].unsqueeze(1).to_broadcast([P, Q, PACK]), ALU.mult,
-        )
-
-        neg_capped = keep.tile([P, PACK, P], F32, name="neg_capped")
-        neg_kept = keep.tile([P, 1], F32, name="neg_kept")
-        nc.scalar.activation(neg_capped[:], capped[:], ACT.Copy, scale=-1.0, accum_out=neg_kept[:])
-
-        weight_words = keep.tile([P, Q], U32, name="weight_words", align_bytes=64)
-        weight_scales = keep.tile([P, Q], U8, name="weight_scales", align_bytes=64)
-        nc.vector.quantize_mx(weight_words[:].bitcast(FP8X4), weight_scales[:], weights_bf[:].rearrange("p q t -> p (q t)"))
+        shares = keep.tile([P, I], F32, name="shares", tag="shares", align_bytes=64)
+        nc.scalar.activation(shares[:], probs[:], ACT.Copy, scale=inv_sum[:])
         left = keep.tile([P, 1], F32, name="left")
-        nc.vector.tensor_scalar(left[:], neg_kept[:], 1.0, None, ALU.add)
+        excess = keep.tile([P, I], F32, name="excess")
+        nc.scalar.activation(excess[:], probs[:], ACT.Relu, bias=neg_cap[:], scale=inv_sum[:], accum_out=left[:])
 
-        stand_flat = stand_rows[:].rearrange("q n j -> q (n j)")
+        grouped2 = keep.tile([P, I], BF16, name="grouped2", align_bytes=64)
+        turn(gather_vals(2, "row_sum"), "bank0", grouped2[:])
 
-        def finish(b):
-            acc = psum.tile([P, P], F32, name="acc", tag="acc", bufs=3)
+        weights = keep.tile([P, I], BF16, name="weights", tag="val_pool2", align_bytes=64)
+        nc.vector.scalar_tensor_tensor(weights[:], shares[:], cols[:, 8:9], size_ps[:], ALU.min, ALU.mult)
+        grouped_w = keep.tile([P, I], BF16, name="grouped_w", align_bytes=64)
+        turn(weights, "bank_w", grouped_w[:])
+
+        stand_ps = psum.tile([P, E], F32, name="stand_ps")
+        for a in range(4):
+            nc.tensor.transpose(stand_ps[:, a * P : (a + 1) * P], cols[:, 4 + a : 5 + a].to_broadcast([P, P]), ident[:])
+        stand_left = keep.tile([P, E], F32, name="stand_left")
+        nc.scalar.activation(stand_left[:], stand_ps[:], ACT.Copy, scale=left[:])
+
+        grouped3 = keep.tile([P, I], BF16, name="grouped3", tag="grouped3", align_bytes=64)
+        turn(gather_vals(3, "shares"), "bank1", grouped3[:])
+
+        words = keep.tile([P, 5 * P], U32, name="words", tag="val_pool3", align_bytes=64)
+        weights_mx = quantize("weights", grouped_w[:], words[:, 4 * P : 5 * P])
+        vals01 = quantize("vals01", grouped01[:], words[:, 0 : 2 * P])
+        vals2 = quantize("vals2", grouped2[:], words[:, 2 * P : 3 * P])
+        vals3 = quantize("vals3", grouped3[:], words[:, 3 * P : 4 * P])
+
+        def multiply(acc, vals_mx):
             nc.tensor.matmul_mx(
-                acc[:], lhsT=weight_words[:].bitcast(FP8X4), lhsT_scale=weight_scales[:],
-                rhs=val_words[b][:].bitcast(FP8X4), rhs_scale=val_scales[b][:], start=True, stop=True,
+                acc, lhsT=weights_mx[0].bitcast(FP8X4), lhsT_scale=weights_mx[1][:],
+                rhs=vals_mx[0].bitcast(FP8X4), rhs_scale=vals_mx[1][:], start=True, stop=True,
             )
-            tag = "grouped%d" % (b + 1) if b + 2 < BLOCKS else "result%d" % b
-            result = keep.tile([P, P], F32, name="result%d" % b, tag=tag, align_bytes=64)
-            nc.vector.scalar_tensor_tensor(
-                result[:], stand_flat[:, b * P : (b + 1) * P], left[:], acc[:], ALU.mult, ALU.add
-            )
-            nc.sync.dma_start(out[:, b * P : (b + 1) * P], result[:])
 
-        grouped2 = gather_vals(2)
-        quantize_vals(1, grouped1)
-        finish(0)
-        grouped3 = gather_vals(3)
-        quantize_vals(2, grouped2)
-        finish(1)
-        finish(2)
-        quantize_vals(3, grouped3)
-        finish(3)
+        def finish(acc, first, width, tag):
+            result = keep.tile([P, width], F32, name="result", tag=tag, align_bytes=64)
+            nc.vector.tensor_tensor(result[:], acc[:], stand_left[:, first : first + width], ALU.add)
+            nc.sync.dma_start(out[:, first : first + width], result[:])
+
+        acc_early = psum.tile([P, 3 * P], F32, name="acc_early")
+        multiply(acc_early[:, 0 : 2 * P], vals01)
+        multiply(acc_early[:, 2 * P : 3 * P], vals2)
+        acc_last = psum.tile([P, P], F32, name="acc_last")
+        multiply(acc_last[:], vals3)
+        finish(acc_early, 0, 3 * P, "grouped3")
+        finish(acc_last, 3 * P, P, "result_last")

@@ -71,7 +71,7 @@ def tile_attend_cappedweights_kernel(tc, query, keys_words, keys_scales, cap, st
 
         query_bf = keep.tile([P, Q, PACK], BF16, name="query_bf", align_bytes=64)
         nc.scalar.copy(query_bf[:], query_raw[:].rearrange("p j q -> p q j"))
-        query_words = keep.tile([P, Q], U32, name="query_words", tag="query_words", align_bytes=64)
+        query_words = keep.tile([P, Q], U32, name="query_words", align_bytes=64)
         query_scales = keep.tile([P, Q], U8, name="query_scales", align_bytes=64)
         nc.vector.quantize_mx(query_words[:].bitcast(FP8X4), query_scales[:], query_bf[:].rearrange("p q j -> p (q j)"))
 
@@ -117,7 +117,7 @@ def tile_attend_cappedweights_kernel(tc, query, keys_words, keys_scales, cap, st
             return words, scales
 
         grouped01 = keep.tile([P, 2 * I], BF16, name="grouped01", align_bytes=64)
-        turn(gather_vals(0, "query_words"), "bank0", grouped01[:, 0:I])
+        turn(gather_vals(0, "picked0"), "bank0", grouped01[:, 0:I])
         turn(gather_vals(1, "key_scales"), "bank1", grouped01[:, I : 2 * I])
 
         inv_sum = keep.tile([P, 1], F32, name="inv_sum", tag="val_pool1", align_bytes=64)
@@ -157,15 +157,15 @@ def tile_attend_cappedweights_kernel(tc, query, keys_words, keys_scales, cap, st
                 rhs=vals_mx[0].bitcast(FP8X4), rhs_scale=vals_mx[1][:], start=True, stop=True,
             )
 
-        def finish(acc, first, width, tag):
+        def finish(acc, first, width, tag, queue):
             result = keep.tile([P, width], F32, name="result", tag=tag, align_bytes=64)
             nc.vector.tensor_tensor(result[:], acc[:], stand_left[:, first : first + width], ALU.add)
-            nc.sync.dma_start(out[:, first : first + width], result[:])
+            queue.dma_start(out[:, first : first + width], result[:])
 
         acc_early = psum.tile([P, 3 * P], F32, name="acc_early")
         multiply(acc_early[:, 0 : 2 * P], vals01)
         multiply(acc_early[:, 2 * P : 3 * P], vals2)
         acc_last = psum.tile([P, P], F32, name="acc_last")
         multiply(acc_last[:], vals3)
-        finish(acc_early, 0, 3 * P, "grouped3")
-        finish(acc_last, 3 * P, P, "result_last")
+        finish(acc_early, 0, 3 * P, "grouped3", nc.sync)
+        finish(acc_last, 3 * P, P, "result_last", nc.scalar)

@@ -28,11 +28,11 @@ def tile_attend_cappedweights_kernel(tc, query, keys_words, keys_scales, cap, st
         keep = ctx.enter_context(tc.tile_pool(name="keep", bufs=1))
         psum = ctx.enter_context(tc.psum_pool(name="psum", bufs=1))
 
-        offsets = keep.tile([P, I // 16], U16, name="offsets")
-        nc.sync.dma_start(offsets[:], offs)
-
         key_word_pool = keep.tile([P, T], I32, name="key_word_pool", align_bytes=64)
         nc.sync.dma_start(key_word_pool[:], keys_words[0].rearrange("p n t -> p (n t)").bitcast(I32))
+
+        offsets = keep.tile([P, I // 16], U16, name="offsets")
+        nc.sync.dma_start(offsets[:], offs)
 
         key_scale_pool = keep.tile([P, T], U8, name="key_scale_pool", align_bytes=64)
         nc.vector.memset(key_scale_pool[:].bitcast(I32), 0)
@@ -83,7 +83,7 @@ def tile_attend_cappedweights_kernel(tc, query, keys_words, keys_scales, cap, st
 
         neg_max = keep.tile([P, 1], F32, name="neg_max")
         nc.vector.tensor_reduce(neg_max[:], scores[:], AX.X, ALU.max, negate=True)
-        probs = keep.tile([P, I], F32, name="probs")
+        probs = keep.tile([P, I], F32, name="probs", tag="probs", align_bytes=64)
         row_sum = keep.tile([P, 1], F32, name="row_sum", tag="row_sum", align_bytes=64)
         nc.scalar.activation(probs[:], scores[:], ACT.Exp, bias=neg_max[:], scale=1.0, accum_out=row_sum[:])
 
@@ -122,7 +122,7 @@ def tile_attend_cappedweights_kernel(tc, query, keys_words, keys_scales, cap, st
 
         inv_sum = keep.tile([P, 1], F32, name="inv_sum", tag="val_pool1", align_bytes=64)
         nc.vector.reciprocal(inv_sum[:], row_sum[:])
-        shares = keep.tile([P, I], F32, name="shares", tag="shares", align_bytes=64)
+        shares = keep.tile([P, I], F32, name="shares")
         nc.scalar.activation(shares[:], probs[:], ACT.Copy, scale=inv_sum[:])
         left = keep.tile([P, 1], F32, name="left")
         excess = keep.tile([P, I], F32, name="excess")
@@ -131,7 +131,7 @@ def tile_attend_cappedweights_kernel(tc, query, keys_words, keys_scales, cap, st
         grouped2 = keep.tile([P, I], BF16, name="grouped2", align_bytes=64)
         turn(gather_vals(2, "row_sum"), "bank0", grouped2[:])
 
-        weights = keep.tile([P, I], BF16, name="weights", tag="val_pool2", align_bytes=64)
+        weights = keep.tile([P, I], BF16, name="weights", align_bytes=64)
         nc.vector.scalar_tensor_tensor(weights[:], shares[:], cols[:, 8:9], size_ps[:], ALU.min, ALU.mult)
         grouped_w = keep.tile([P, I], BF16, name="grouped_w", align_bytes=64)
         turn(weights, "bank_w", grouped_w[:])
@@ -143,7 +143,7 @@ def tile_attend_cappedweights_kernel(tc, query, keys_words, keys_scales, cap, st
         nc.scalar.activation(stand_left[:], stand_ps[:], ACT.Copy, scale=left[:])
 
         grouped3 = keep.tile([P, I], BF16, name="grouped3", tag="grouped3", align_bytes=64)
-        turn(gather_vals(3, "shares"), "bank1", grouped3[:])
+        turn(gather_vals(3, "probs"), "bank1", grouped3[:])
 
         words = keep.tile([P, 5 * P], U32, name="words", tag="val_pool3", align_bytes=64)
         weights_mx = quantize("weights", grouped_w[:], words[:, 4 * P : 5 * P])

from contextlib import ExitStack

import concourse.mybir as mybir
from concourse.masks import make_identity

D, T, I, Q, E = 512, 2048, 512, 128, 512
FLOPS = 2 * Q * I * D + 2 * Q * E * I

F32 = mybir.dt.float32
BF16 = mybir.dt.bfloat16
I32 = mybir.dt.int32
U32 = mybir.dt.uint32
U16 = mybir.dt.uint16
U8 = mybir.dt.uint8
FP8X4 = mybir.dt.float8_e4m3fn_x4
ALU = mybir.AluOpType
ACT = mybir.ActivationFunctionType
AX = mybir.AxisListType

P = 128
PACK = 4
BLOCKS = E // P


def tile_attend_cappedweights_kernel(tc, query, keys_words, keys_scales, cap, stand, size, vals, offs, out):
    nc = tc.nc
    with ExitStack() as ctx:
        keep = ctx.enter_context(tc.tile_pool(name="keep", bufs=1))
        psum = ctx.enter_context(tc.psum_pool(name="psum", bufs=1))

        key_word_pool = keep.tile([P, T], I32, name="key_word_pool", align_bytes=64)
        nc.sync.dma_start(key_word_pool[:], keys_words[0].rearrange("p n t -> p (n t)").bitcast(I32))

        offsets = keep.tile([P, I // 16], U16, name="offsets")
        nc.sync.dma_start(offsets[:], offs)

        key_scale_pool = keep.tile([P, T], U8, name="key_scale_pool", align_bytes=64)
        nc.vector.memset(key_scale_pool[:].bitcast(I32), 0)
        scale_rows = keys_scales[0].bitcast(I32)
        for quad in (0, 2, 1, 3):
            nc.sync.dma_start(
                key_scale_pool[32 * quad : 32 * quad + 4, :].bitcast(I32), scale_rows[4 * quad : 4 * quad + 4, :]
            )

        query_raw = keep.tile([P, PACK, Q], F32, name="query_raw")
        nc.sync.dma_start(query_raw[:], query.rearrange("(p j) q -> p j q", j=PACK))

        val_pool = []

        def load_vals(b):
            pool_b = keep.tile([P, T], F32, name="val_pool%d" % b, tag="val_pool%d" % b, align_bytes=64)
            nc.sync.dma_start(pool_b[:], vals[b * P : (b + 1) * P, :])
            val_pool.append(pool_b)

        load_vals(0)
        rows = keep.tile([P, P], F32, name="rows")
        nc.gpsimd.memset(rows[:], 0.0)
        nc.sync.dma_start(rows[8:9, :], cap.rearrange("q o -> o q"))
        nc.sync.dma_start(rows[0:4, :], size.rearrange("o (a n) -> (o a) n", a=4))
        nc.sync.dma_start(rows[4:8, :], stand.rearrange("o (a n) -> (o a) n", a=4))
        for b in range(1, BLOCKS):
            load_vals(b)

        ident = keep.tile([P, P], F32, name="ident")
        make_identity(nc, ident[:])

        key_words = keep.tile([P, I], U32, name="key_words", align_bytes=64)
        nc.vector.tensor_copy(key_words[:], key_word_pool[:].bitcast(U32).indirect(offsets[:]))
        key_scales = keep.tile([P, I], U8, name="key_scales", tag="key_scales", align_bytes=64)
        nc.vector.tensor_copy(key_scales[:], key_scale_pool[:].indirect(offsets[:]))

        query_bf = keep.tile([P, Q, PACK], BF16, name="query_bf", align_bytes=64)
        nc.scalar.copy(query_bf[:], query_raw[:].rearrange("p j q -> p q j"))
        query_words = keep.tile([P, Q], U32, name="query_words", align_bytes=64)
        query_scales = keep.tile([P, Q], U8, name="query_scales", align_bytes=64)
        nc.vector.quantize_mx(query_words[:].bitcast(FP8X4), query_scales[:], query_bf[:].rearrange("p q j -> p (q j)"))

        scores = psum.tile([P, I], F32, name="scores")
        nc.tensor.matmul_mx(
            scores[:], lhsT=query_words[:].bitcast(FP8X4), lhsT_scale=query_scales[:],
            rhs=key_words[:].bitcast(FP8X4), rhs_scale=key_scales[:], start=True, stop=True,
        )

        neg_max = keep.tile([P, 1], F32, name="neg_max")
        nc.vector.tensor_reduce(neg_max[:], scores[:], AX.X, ALU.max, negate=True)
        probs = keep.tile([P, I], F32, name="probs", tag="probs", align_bytes=64)
        row_sum = keep.tile([P, 1], F32, name="row_sum", tag="row_sum", align_bytes=64)
        nc.scalar.activation(probs[:], scores[:], ACT.Exp, bias=neg_max[:], scale=1.0, accum_out=row_sum[:])

        rows_t = psum.tile([P, P], F32, name="rows_t", tag="bank0")
        nc.tensor.transpose(rows_t[:], rows[:], ident[:])
        cols = keep.tile([P, 16], F32, name="cols")
        nc.scalar.copy(cols[:], rows_t[:, 0:16])
        neg_cap = keep.tile([P, 1], F32, name="neg_cap")
        nc.scalar.activation(neg_cap[:], rows_t[:, 8:9], ACT.Copy, scale=-1.0)
        size_ps = psum.tile([P, I], F32, name="size_ps")
        for a in range(4):
            nc.tensor.transpose(size_ps[:, a * P : (a + 1) * P], cols[:, a : a + 1].to_broadcast([P, P]), ident[:])

        def turn(flat, bank, grouped):
            pairs = flat[:].bitcast(F32)
            turned = psum.tile([P, 2, P], F32, name="turned", tag=bank)
            for u in range(2):
                nc.tensor.transpose(turned[:, u, :], pairs[:, u : I // 2 : 2], ident[:])
            nc.scalar.copy(
                grouped.bitcast(F32).rearrange("p (e u) -> p e u", u=2), turned[:].rearrange("p u e -> p e u")
            )

        def gather_vals(b, tag):
            picked = keep.tile([P, I], BF16, name="picked%d" % b, tag=tag, align_bytes=64)
            nc.vector.tensor_copy(picked[:], val_pool[b][:].indirect(offsets[:]))
            return picked

        def quantize(name, grouped, words):
            scales = keep.tile(list(words.shape), U8, name=name + "_scales", align_bytes=64)
            nc.vector.quantize_mx(words.bitcast(FP8X4), scales[:], grouped)
            return words, scales

        grouped01 = keep.tile([P, 2 * I], BF16, name="grouped01", align_bytes=64)
        turn(gather_vals(0, "picked0"), "bank0", grouped01[:, 0:I])
        turn(gather_vals(1, "key_scales"), "bank1", grouped01[:, I : 2 * I])

        inv_sum = keep.tile([P, 1], F32, name="inv_sum", tag="val_pool1", align_bytes=64)
        nc.vector.reciprocal(inv_sum[:], row_sum[:])
        shares = keep.tile([P, I], F32, name="shares")
        nc.scalar.activation(shares[:], probs[:], ACT.Copy, scale=inv_sum[:])
        left = keep.tile([P, 1], F32, name="left")
        excess = keep.tile([P, I], F32, name="excess")
        nc.scalar.activation(excess[:], probs[:], ACT.Relu, bias=neg_cap[:], scale=inv_sum[:], accum_out=left[:])

        grouped2 = keep.tile([P, I], BF16, name="grouped2", align_bytes=64)
        turn(gather_vals(2, "row_sum"), "bank0", grouped2[:])

        weights = keep.tile([P, I], BF16, name="weights", align_bytes=64)
        nc.vector.scalar_tensor_tensor(weights[:], shares[:], cols[:, 8:9], size_ps[:], ALU.min, ALU.mult)
        grouped_w = keep.tile([P, I], BF16, name="grouped_w", align_bytes=64)
        turn(weights, "bank_w", grouped_w[:])

        stand_ps = psum.tile([P, E], F32, name="stand_ps")
        for a in range(4):
            nc.tensor.transpose(stand_ps[:, a * P : (a + 1) * P], cols[:, 4 + a : 5 + a].to_broadcast([P, P]), ident[:])
        stand_left = keep.tile([P, E], F32, name="stand_left")
        nc.scalar.activation(stand_left[:], stand_ps[:], ACT.Copy, scale=left[:])

        grouped3 = keep.tile([P, I], BF16, name="grouped3", tag="grouped3", align_bytes=64)
        turn(gather_vals(3, "probs"), "bank1", grouped3[:])

        words = keep.tile([P, 5 * P], U32, name="words", tag="val_pool3", align_bytes=64)
        weights_mx = quantize("weights", grouped_w[:], words[:, 4 * P : 5 * P])
        vals01 = quantize("vals01", grouped01[:], words[:, 0 : 2 * P])
        vals2 = quantize("vals2", grouped2[:], words[:, 2 * P : 3 * P])
        vals3 = quantize("vals3", grouped3[:], words[:, 3 * P : 4 * P])

        def multiply(acc, vals_mx):
            nc.tensor.matmul_mx(
                acc, lhsT=weights_mx[0].bitcast(FP8X4), lhsT_scale=weights_mx[1][:],
                rhs=vals_mx[0].bitcast(FP8X4), rhs_scale=vals_mx[1][:], start=True, stop=True,
            )

        def finish(acc, first, width, tag, queue):
            result = keep.tile([P, width], F32, name="result", tag=tag, align_bytes=64)
            nc.vector.tensor_tensor(result[:], acc[:], stand_left[:, first : first + width], ALU.add)
            queue.dma_start(out[:, first : first + width], result[:])

        acc_early = psum.tile([P, 3 * P], F32, name="acc_early")
        multiply(acc_early[:, 0 : 2 * P], vals01)
        multiply(acc_early[:, 2 * P : 3 * P], vals2)
        acc_last = psum.tile([P, P], F32, name="acc_last")
        multiply(acc_last[:], vals3)
        finish(acc_early, 0, 3 * P, "grouped3", nc.sync)
        finish(acc_last, 3 * P, P, "result_last", nc.scalar)
